import numpy as np
import ml_dtypes

BF16 = ml_dtypes.bfloat16


def bf(x):
    return np.asarray(x, np.float32).astype(BF16)


def f32(x):
    return np.asarray(x, np.float32)


def f64(x):
    return np.asarray(x).astype(np.float64)


def striped(idx):
    return np.tile(idx.reshape(-1, 16).T, (8, 1))


def rows(idx, k):
    return np.tile(idx, (k, 1))


def look(tab, idx):
    return np.take_along_axis(f64(tab), rows(idx, len(tab)), axis=1)


K, S, H, D, V, N = 256, 2048, 256, 2, 512, 1024


def setup_inputs():
    return {"z": bf(np.random.standard_normal((H, S))), "wt": bf(np.random.standard_normal((H, K)) / np.sqrt(H)), "x0": f32(1.0 * np.random.standard_normal((K, V))), "offs": striped(np.random.permutation(S)[:N])}


def reference(z, wt, x0, offs):
    idx = offs[:16].T.reshape(-1)
    tab = f64(wt).T @ f64(z)
    x = f64(x0)
    for d in range(D):
        x = np.maximum(x, look(tab, idx[d * V:(d + 1) * V]))
    return x

@@ -1,0 +1,62 @@
+import concourse.mybir as mybir
+
+BF16, F32, U16 = mybir.dt.bfloat16, mybir.dt.float32, mybir.dt.uint16
+
+P = 128
+K, S, H, V, D = 256, 2048, 256, 512, 2
+BANK = 512
+
+FLOPS = 2 * H * K * S
+
+
+def tile_lookup_pjmax_out_kernel(tc, z, wt, x0, offs, out):
+    nc = tc.nc
+    n_feature_blocks, n_row_blocks, n_chunks = H // P, K // P, S // BANK
+    half = S // 2
+    with (
+        tc.tile_pool(name="held", bufs=1) as held,
+        tc.psum_pool(name="psum", bufs=8) as psum,
+    ):
+        weights = held.tile([P, n_feature_blocks, K], BF16, name="weights")
+        nc.sync.dma_start(weights[:], wt.rearrange("(f p) r -> p f r", p=P))
+        z_by_half = []
+        z_view = z.rearrange("(f p) s -> p f s", p=P)
+        for h in range(2):
+            z_half = held.tile([P, n_feature_blocks, half], BF16, name=f"z_half{h}")
+            queue = nc.sync if h == 0 else nc.scalar
+            queue.dma_start(z_half[:], z_view[:, :, h * half:(h + 1) * half])
+            z_by_half.append(z_half)
+
+        offsets = held.tile([P, D * V // 16], U16, name="offsets")
+        nc.sync.dma_start(offsets[:], offs)
+        columns = V // 16
+        own_values = []
+        for r in range(n_row_blocks):
+            own = held.tile([P, V], F32, name=f"own{r}")
+            nc.sync.dma_start(own[:], x0[r * P:(r + 1) * P, :])
+            own_values.append(own)
+
+        for r in range(n_row_blocks):
+            rows = slice(r * P, (r + 1) * P)
+            table = held.tile([P, S], F32, name=f"table{r}")
+            for c in range(n_chunks):
+                bank = psum.tile([P, BANK], F32, name="bank")
+                z_half = z_by_half[c * BANK // half]
+                start = c * BANK % half
+                for f in range(n_feature_blocks):
+                    nc.tensor.matmul(
+                        bank[:], weights[:, f, rows], z_half[:, f, start:start + BANK],
+                        start=(f == 0), stop=(f == n_feature_blocks - 1),
+                    )
+                if r == 0 and c % 2 == 1:
+                    nc.vector.tensor_copy(table[:, c * BANK:(c + 1) * BANK], bank[:])
+                else:
+                    nc.scalar.copy(table[:, c * BANK:(c + 1) * BANK], bank[:])
+
+            largest = own_values[r]
+            for d in range(D):
+                larger = held.tile([P, V], F32, name=f"larger{r}_{d}")
+                neighbours = table[:].indirect(offsets[:, d * columns:(d + 1) * columns])
+                nc.vector.tensor_tensor(larger[:], neighbours, largest[:], mybir.AluOpType.max)
+                largest = larger
+            nc.sync.dma_start(out[rows, :], largest[:])

@@ -11,25 +11,32 @@ FLOPS = 2 * H * K * S
 
 def tile_lookup_pjmax_out_kernel(tc, z, wt, x0, offs, out):
     nc = tc.nc
-    n_feature_blocks, n_row_blocks, n_chunks = H // P, K // P, S // BANK
-    half = S // 2
+    n_feature_blocks, n_row_blocks, n_halves = H // P, K // P, 2
+    half = S // n_halves
+    n_warm_up = 4
     with (
         tc.tile_pool(name="held", bufs=1) as held,
         tc.psum_pool(name="psum", bufs=8) as psum,
     ):
+        zeros = held.tile([P, BANK], BF16, name="zeros")
+        nc.vector.memset(zeros[:], 0.0)
+        idle_bank = psum.tile([P, BANK], F32, tag="bank", name="idle_bank")
+        for u in range(n_warm_up):
+            nc.tensor.matmul(idle_bank[:], zeros[:, :P], zeros[:], start=True, stop=True)
+
         weights = held.tile([P, n_feature_blocks, K], BF16, name="weights")
-        nc.sync.dma_start(weights[:], wt.rearrange("(f p) r -> p f r", p=P))
-        z_by_half = []
-        z_view = z.rearrange("(f p) s -> p f s", p=P)
-        for h in range(2):
-            z_half = held.tile([P, n_feature_blocks, half], BF16, name=f"z_half{h}")
-            queue = nc.sync if h == 0 else nc.scalar
-            queue.dma_start(z_half[:], z_view[:, :, h * half:(h + 1) * half])
-            z_by_half.append(z_half)
+        nc.scalar.dma_start(weights[:], wt.rearrange("(f p) r -> p f r", p=P))
+        queues = [nc.sync, nc.scalar]
+        places = {}
+        for h in range(n_halves):
+            for f in range(n_feature_blocks):
+                places[f, h] = held.tile([P, half], BF16, name=f"z{f}_{h}")
+                queues[f].dma_start(places[f, h][:], z[f * P:(f + 1) * P, h * half:(h + 1) * half])
 
         offsets = held.tile([P, D * V // 16], U16, name="offsets")
         nc.sync.dma_start(offsets[:], offs)
-        columns = V // 16
+        n_groups = 2
+        group = V // n_groups
         own_values = []
         for r in range(n_row_blocks):
             own = held.tile([P, V], F32, name=f"own{r}")
@@ -39,24 +46,27 @@ def tile_lookup_pjmax_out_kernel(tc, z, wt, x0, offs, out):
         for r in range(n_row_blocks):
             rows = slice(r * P, (r + 1) * P)
             table = held.tile([P, S], F32, name=f"table{r}")
-            for c in range(n_chunks):
+            for c in range(S // BANK):
+                h, start = divmod(c * BANK, half)
                 bank = psum.tile([P, BANK], F32, name="bank")
-                z_half = z_by_half[c * BANK // half]
-                start = c * BANK % half
                 for f in range(n_feature_blocks):
                     nc.tensor.matmul(
-                        bank[:], weights[:, f, rows], z_half[:, f, start:start + BANK],
+                        bank[:], weights[:, f, rows], places[f, h][:, start:start + BANK],
                         start=(f == 0), stop=(f == n_feature_blocks - 1),
                     )
+                piece = table[:, c * BANK:(c + 1) * BANK]
                 if r == 0 and c % 2 == 1:
-                    nc.vector.tensor_copy(table[:, c * BANK:(c + 1) * BANK], bank[:])
+                    nc.vector.tensor_copy(piece, bank[:])
                 else:
-                    nc.scalar.copy(table[:, c * BANK:(c + 1) * BANK], bank[:])
+                    nc.scalar.copy(piece, bank[:])
 
-            largest = own_values[r]
+            largest = [own_values[r][:, g * group:(g + 1) * group] for g in range(n_groups)]
             for d in range(D):
-                larger = held.tile([P, V], F32, name=f"larger{r}_{d}")
-                neighbours = table[:].indirect(offsets[:, d * columns:(d + 1) * columns])
-                nc.vector.tensor_tensor(larger[:], neighbours, largest[:], mybir.AluOpType.max)
-                largest = larger
-            nc.sync.dma_start(out[rows, :], largest[:])
+                for g in range(n_groups):
+                    larger = held.tile([P, group], F32, name=f"larger{r}_{d}_{g}")
+                    first = (d * V + g * group) // 16
+                    neighbours = table[:].indirect(offsets[:, first:first + group // 16])
+                    nc.vector.tensor_tensor(larger[:], neighbours, largest[g], mybir.AluOpType.max)
+                    largest[g] = larger[:]
+            for g in range(n_groups):
+                nc.sync.dma_start(out[rows, g * group:(g + 1) * group], largest[g])

@@ -11,9 +11,8 @@ FLOPS = 2 * H * K * S
 
 def tile_lookup_pjmax_out_kernel(tc, z, wt, x0, offs, out):
     nc = tc.nc
-    n_feature_blocks, n_row_blocks, n_halves = H // P, K // P, 2
-    half = S // n_halves
-    n_warm_up = 4
+    n_feature_blocks, n_row_blocks, n_chunks = H // P, K // P, S // BANK
+    n_warm_up = 3
     with (
         tc.tile_pool(name="held", bufs=1) as held,
         tc.psum_pool(name="psum", bufs=8) as psum,
@@ -26,12 +25,12 @@ def tile_lookup_pjmax_out_kernel(tc, z, wt, x0, offs, out):
 
         weights = held.tile([P, n_feature_blocks, K], BF16, name="weights")
         nc.scalar.dma_start(weights[:], wt.rearrange("(f p) r -> p f r", p=P))
-        queues = [nc.sync, nc.scalar]
-        places = {}
-        for h in range(n_halves):
-            for f in range(n_feature_blocks):
-                places[f, h] = held.tile([P, half], BF16, name=f"z{f}_{h}")
-                queues[f].dma_start(places[f, h][:], z[f * P:(f + 1) * P, h * half:(h + 1) * half])
+        z_view = z.rearrange("(f p) s -> p f s", p=P)
+        places = []
+        for c in range(n_chunks):
+            chunk = held.tile([P, n_feature_blocks, BANK], BF16, name=f"z{c}")
+            nc.sync.dma_start(chunk[:], z_view[:, :, c * BANK:(c + 1) * BANK])
+            places.append(chunk)
 
         offsets = held.tile([P, D * V // 16], U16, name="offsets")
         nc.sync.dma_start(offsets[:], offs)
@@ -46,16 +45,15 @@ def tile_lookup_pjmax_out_kernel(tc, z, wt, x0, offs, out):
         for r in range(n_row_blocks):
             rows = slice(r * P, (r + 1) * P)
             table = held.tile([P, S], F32, name=f"table{r}")
-            for c in range(S // BANK):
-                h, start = divmod(c * BANK, half)
+            for c in range(n_chunks):
                 bank = psum.tile([P, BANK], F32, name="bank")
                 for f in range(n_feature_blocks):
                     nc.tensor.matmul(
-                        bank[:], weights[:, f, rows], places[f, h][:, start:start + BANK],
+                        bank[:], weights[:, f, rows], places[c][:, f, :],
                         start=(f == 0), stop=(f == n_feature_blocks - 1),
                     )
                 piece = table[:, c * BANK:(c + 1) * BANK]
-                if r == 0 and c % 2 == 1:
+                if r == 0 and c % 2 == 0:
                     nc.vector.tensor_copy(piece, bank[:])
                 else:
                     nc.scalar.copy(piece, bank[:])

@@ -45,14 +45,16 @@ def tile_lookup_pjmax_out_kernel(tc, z, wt, x0, offs, out):
         for r in range(n_row_blocks):
             rows = slice(r * P, (r + 1) * P)
             table = held.tile([P, S], F32, name=f"table{r}")
-            for c in range(n_chunks):
-                bank = psum.tile([P, BANK], F32, name="bank")
+            width = BANK // 2 if r == 0 else BANK
+            for c in range(S // width):
+                bank = psum.tile([P, width], F32, tag="bank", name="bank")
+                start = c * width % BANK
                 for f in range(n_feature_blocks):
                     nc.tensor.matmul(
-                        bank[:], weights[:, f, rows], places[c][:, f, :],
+                        bank[:], weights[:, f, rows], places[c * width // BANK][:, f, start:start + width],
                         start=(f == 0), stop=(f == n_feature_blocks - 1),
                     )
-                piece = table[:, c * BANK:(c + 1) * BANK]
+                piece = table[:, c * width:(c + 1) * width]
                 if r == 0 and c % 2 == 0:
                     nc.vector.tensor_copy(piece, bank[:])
                 else:

import concourse.mybir as mybir

BF16, F32, U16 = mybir.dt.bfloat16, mybir.dt.float32, mybir.dt.uint16

P = 128
K, S, H, V, D = 256, 2048, 256, 512, 2
BANK = 512

FLOPS = 2 * H * K * S


def tile_lookup_pjmax_out_kernel(tc, z, wt, x0, offs, out):
    nc = tc.nc
    n_feature_blocks, n_row_blocks, n_chunks = H // P, K // P, S // BANK
    n_warm_up = 3
    with (
        tc.tile_pool(name="held", bufs=1) as held,
        tc.psum_pool(name="psum", bufs=8) as psum,
    ):
        zeros = held.tile([P, BANK], BF16, name="zeros")
        nc.vector.memset(zeros[:], 0.0)
        idle_bank = psum.tile([P, BANK], F32, tag="bank", name="idle_bank")
        for u in range(n_warm_up):
            nc.tensor.matmul(idle_bank[:], zeros[:, :P], zeros[:], start=True, stop=True)

        weights = held.tile([P, n_feature_blocks, K], BF16, name="weights")
        nc.scalar.dma_start(weights[:], wt.rearrange("(f p) r -> p f r", p=P))
        z_view = z.rearrange("(f p) s -> p f s", p=P)
        places = []
        for c in range(n_chunks):
            chunk = held.tile([P, n_feature_blocks, BANK], BF16, name=f"z{c}")
            nc.sync.dma_start(chunk[:], z_view[:, :, c * BANK:(c + 1) * BANK])
            places.append(chunk)

        offsets = held.tile([P, D * V // 16], U16, name="offsets")
        nc.sync.dma_start(offsets[:], offs)
        n_groups = 2
        group = V // n_groups
        own_values = []
        for r in range(n_row_blocks):
            own = held.tile([P, V], F32, name=f"own{r}")
            nc.sync.dma_start(own[:], x0[r * P:(r + 1) * P, :])
            own_values.append(own)

        for r in range(n_row_blocks):
            rows = slice(r * P, (r + 1) * P)
            table = held.tile([P, S], F32, name=f"table{r}")
            width = BANK // 2 if r == 0 else BANK
            for c in range(S // width):
                bank = psum.tile([P, width], F32, tag="bank", name="bank")
                start = c * width % BANK
                for f in range(n_feature_blocks):
                    nc.tensor.matmul(
                        bank[:], weights[:, f, rows], places[c * width // BANK][:, f, start:start + width],
                        start=(f == 0), stop=(f == n_feature_blocks - 1),
                    )
                piece = table[:, c * width:(c + 1) * width]
                if r == 0 and c % 2 == 0:
                    nc.vector.tensor_copy(piece, bank[:])
                else:
                    nc.scalar.copy(piece, bank[:])

            largest = [own_values[r][:, g * group:(g + 1) * group] for g in range(n_groups)]
            for d in range(D):
                for g in range(n_groups):
                    larger = held.tile([P, group], F32, name=f"larger{r}_{d}_{g}")
                    first = (d * V + g * group) // 16
                    neighbours = table[:].indirect(offsets[:, first:first + group // 16])
                    nc.vector.tensor_tensor(larger[:], neighbours, largest[g], mybir.AluOpType.max)
                    largest[g] = larger[:]
            for g in range(n_groups):
                nc.sync.dma_start(out[rows, g * group:(g + 1) * group], largest[g])
